import numpy as np
import ml_dtypes


def mxq(x, axis, fmt="e4m3"):
    dtype, down = {"e4m3": (ml_dtypes.float8_e4m3fn, 7), "e5m2": (ml_dtypes.float8_e5m2, 14)}[fmt]
    v = np.moveaxis(np.asarray(x, np.float32).astype(ml_dtypes.bfloat16).astype(np.float64), axis, -1)
    blocks = v.reshape(v.shape[:-1] + (-1, 32))
    amax = np.abs(blocks).max(-1, keepdims=True)
    byte = np.maximum(np.where(amax > 0, np.frexp(amax)[1] - 1 + 127, 0) - down, 1)
    scale = np.exp2(byte - 127.0)
    codes = (blocks / scale).astype(np.float32).astype(dtype).astype(np.float64)
    return np.moveaxis((codes * scale).reshape(v.shape), -1, axis)


WIDE = False


def mx_kscale(k):
    if not WIDE:
        return np.ones(k)
    levels = np.array([10, -10, 5, -5, 0])
    if k % 512:
        return np.exp2(np.random.permutation(np.resize(levels, k // 32))).repeat(32)
    a = np.empty((k // 512, 16))
    for p in range(k // 512):
        a[p, :8] = np.random.permutation(np.resize(levels, 8))
        for g in range(8):
            far = levels[np.abs(levels - a[p, g]) >= 10]
            a[p, g + 8] = far[np.random.randint(len(far))]
    return np.exp2(a.ravel()).repeat(32)


BF16 = ml_dtypes.bfloat16


def bf(x):
    return np.asarray(x, np.float32).astype(BF16)


def f64(x):
    return np.asarray(x).astype(np.float64)


S, R, H, E = 2, 512, 4, 128
D = H * E
EPS = 1e-5


def gain_layer_norm(x, gain):
    mean = np.mean(x, axis=-1, keepdims=True)
    var = np.mean(np.square(x - mean), axis=-1, keepdims=True)
    return (x - mean) / np.sqrt(var + EPS) * gain


def sigmoid(v):
    return 1.0 / (1.0 + np.exp(-v))


def softmax(v):
    e = np.exp(v - v.max(-1, keepdims=True))
    return e / e.sum(-1, keepdims=True)


def draw0():
    f = mx_kscale(D)
    q = mx_kscale(R)
    size = np.exp2(-8.0 * np.random.random_sample((S, R, 1)))
    return {
        "m": bf((0.5 + 1.5 * np.random.standard_normal((S, R, D))) * size),
        "ln_g": bf((1.0 + 0.1 * np.random.standard_normal(D)) * f),
        "w_v": bf(np.random.standard_normal((D, D)) / np.sqrt(D) / f[:, None]),
        "w_g": bf(np.random.standard_normal((D, D)) / np.sqrt(D) / f[:, None]),
        "t": bf((0.5 + np.random.random_sample((S, R))) / q[None, :]),
        "z": bf(np.random.standard_normal((H, R, R)) * 1.5),
        "c": bf(np.random.standard_normal((H, R)) * 0.265 * np.sqrt(R) * q[None, :]),
    }


def core(m, ln_g, w_v, w_g, t, z, c):
    mn = gain_layer_norm(f64(m), f64(ln_g))
    mnq = mxq(mn, 2, "e4m3")
    g = sigmoid(mnq @ mxq(f64(w_g), 0, "e4m3")).reshape(S, R, H, E)
    v0 = (mnq @ mxq(f64(w_v), 0, "e4m3")).reshape(S, R, H, E)
    v = v0 * f64(t)[:, :, None, None]
    p = softmax(f64(z))
    a = p * f64(c)[:, None, :]
    vh = v.transpose(2, 1, 0, 3).reshape(H, R, S * E)
    uh = mxq(a, 2, "e4m3") @ mxq(vh, 1, "e4m3")
    u = uh.reshape(H, R, S, E).transpose(2, 1, 0, 3)
    return (g * u).reshape(S, R, D)


def e4m3fn_bytes(y):
    return np.clip(np.asarray(y, np.float64), -448.0, 448.0).astype(np.float32).astype(ml_dtypes.float8_e4m3fn).view(np.uint8)


def e4m3fn_values(b):
    return np.asarray(b, np.uint8).view(ml_dtypes.float8_e4m3fn).astype(np.float64)


def setup_inputs():
    d = draw0()
    x0 = np.asarray(d['w_v']).astype(np.float64)
    s = (np.max(np.abs(x0), axis=(1,), keepdims=True) / 448.0).astype(np.float32)
    out = {}
    for k, v in d.items():
        if k == 'w_v':
            out['w_v_bytes'] = e4m3fn_bytes(x0 / s.astype(np.float64))
            out['w_v_scale'] = s
        else:
            out[k] = v
    return out


def reference(m, ln_g, w_v_bytes, w_v_scale, w_g, t, z, c):
    return core(m, ln_g, e4m3fn_values(w_v_bytes) * w_v_scale.astype(np.float64), w_g, t, z, c)

@@ -1,0 +1,308 @@
+from contextlib import ExitStack
+
+import concourse.mybir as mybir
+from concourse.masks import make_identity
+
+F32 = mybir.dt.float32
+BF16 = mybir.dt.bfloat16
+U32 = mybir.dt.uint32
+U8 = mybir.dt.uint8
+FP8 = mybir.dt.float8_e4m3fn
+FP8X4 = mybir.dt.float8_e4m3fn_x4
+ACT = mybir.ActivationFunctionType
+ALU = mybir.AluOpType
+AX = mybir.AxisListType
+
+P = 128
+S = 2
+R = 512
+H = 4
+E = 128
+D = H * E
+T = 4
+EPS = 1e-5
+
+FLOPS = 2 * 2 * S * R * D * D + 2 * H * R * R * S * E
+
+
+def tile_msapairweightedaveraging_kernel(tc, m, ln_g, w_v_bytes, w_v_scale, w_g, t, z, c, out):
+    nc = tc.nc
+
+    with ExitStack() as ctx:
+        keep = ctx.enter_context(tc.tile_pool(name="keep", bufs=1))
+        ps_c = ctx.enter_context(tc.psum_pool(name="ps_c", bufs=1))
+        ps_t = ctx.enter_context(tc.psum_pool(name="ps_t", bufs=2))
+        ps_m = ctx.enter_context(tc.psum_pool(name="ps_m", bufs=4))
+
+        def sb(shape, dtype, name):
+            return keep.tile(shape, dtype, name=name, align_bytes=64)
+
+
+        x = [sb([P, T, D], BF16, "x%d" % s) for s in range(S)]
+        zt = [sb([P, H, R], BF16, "z%d" % i) for i in range(T)]
+        wg_raw = sb([P, T, D], BF16, "wg_raw")
+        wv_bytes = sb([P, T, D], U8, "wv_bytes")
+        cst = sb([P, D], BF16, "cst")
+        sv = sb([P, T], F32, "sv")
+        tv = sb([P, S, T], BF16, "tv")
+        gain = sb([P, T], BF16, "gain")
+
+        nc.vector.memset(cst[:], 0.0)
+        mv_ = [m[s].rearrange("(p t) f -> p t f", t=T) for s in range(S)]
+        zv = z.rearrange("h (p t) j -> t p h j", t=T)
+        for k in range(2):
+            nc.sync.dma_start(out=x[0][:, 2 * k : 2 * k + 2, :], in_=mv_[0][:, 2 * k : 2 * k + 2, :])
+        nc.scalar.dma_start(out=cst[0:4, :], in_=c)
+        nc.scalar.dma_start(out=sv[:], in_=w_v_scale.rearrange("(p t) o -> p (t o)", t=T))
+        nc.scalar.dma_start(out=gain[:], in_=ln_g.rearrange("(p t) -> p t", t=T))
+        nc.scalar.dma_start(out=tv[:], in_=t.rearrange("s (p t) -> p s t", t=T))
+        nc.sync.dma_start(out=zt[0][:], in_=zv[0])
+        nc.sync.dma_start(out=x[1][:], in_=mv_[1])
+        nc.sync.dma_start(out=zt[1][:], in_=zv[1])
+        nc.sync.dma_start(out=wv_bytes[:], in_=w_v_bytes.rearrange("(p t) n -> p t n", t=T))
+        nc.sync.dma_start(out=zt[2][:], in_=zv[2])
+        nc.sync.dma_start(out=wg_raw[:], in_=w_g.rearrange("(p t) n -> p t n", t=T))
+        nc.sync.dma_start(out=zt[3][:], in_=zv[3])
+
+        warm = sb([P, 1], F32, "warm")
+        nc.vector.memset(warm[:], 0.0)
+        nc.scalar.activation(out=warm[:], in_=warm[:], func=ACT.Exp)
+        ident = sb([P, P], F32, "ident")
+        make_identity(nc, ident[:])
+        mhalf = sb([P, T], F32, "mhalf")
+        nc.gpsimd.memset(mhalf[:], -0.5)
+        sel = sb([P, 8], BF16, "sel")
+        nc.vector.tensor_copy(out=sel[:], in_=ident[:, 0:8])
+        th = sb([P, S, T], F32, "th")
+        cb = [ps_c.tile([P, 2, R], BF16, name="cb%d" % k) for k in range(2)]
+
+        def weave(*lanes):
+            lanes = [list(l) for l in lanes]
+            while any(lanes):
+                for l in lanes:
+                    if l:
+                        l[0]()
+                        l.remove(l[0])
+
+        def run(*lanes):
+            for l in lanes:
+                for step in l:
+                    step()
+
+        def spread(h):
+            nc.tensor.matmul(cb[h // 2][:, h % 2, :], lhsT=sel[:, h : h + 1].to_broadcast([P, P]), rhs=cst[:], start=True, stop=True)
+
+        def quantize(codes, scales, src):
+            nc.vector.quantize_mx(out=codes.bitcast(FP8X4), scales=scales, in_=src)
+
+        st = [sb([P, T, 6], F32, "st%d" % s) for s in range(S)]
+        mv = [sb([P, T, 2], F32, "mv%d" % s) for s in range(S)]
+        ve = [sb([P, T], F32, "ve%d" % s) for s in range(S)]
+        nmean = [sb([P, T], F32, "nmean%d" % s) for s in range(S)]
+        rstd = [sb([P, T], F32, "rstd%d" % s) for s in range(S)]
+        xn = [sb([P, T, D], F32, "xn%d" % s) for s in range(S)]
+        mg = [sb([P, T * P * T], BF16, "mg%d" % s) for s in range(S)]
+        mq = [sb([P, R], U32, "mq%d" % s) for s in range(S)]
+        ms = [sb([P, R], U8, "ms%d" % s) for s in range(S)]
+
+        def ln_stats(s):
+            def bn(k):
+                return lambda: nc.vector.bn_stats(out=st[s][:, k, :], in_=x[s][:, k, :])
+
+            def agg(k):
+                return lambda: nc.vector.bn_aggr(out=mv[s][:, k, :], in_=st[s][:, k, :])
+
+            return [bn(k) for k in range(T)] + [agg(k) for k in range(T)]
+
+        def ln_scales(s):
+            nc.gpsimd.tensor_scalar(out=ve[s][:], in0=mv[s][:, :, 1], scalar1=1.0, scalar2=EPS, op0=ALU.mult, op1=ALU.add)
+            nc.gpsimd.tensor_tensor(out=rstd[s][:], in0=ve[s][:], in1=mhalf[:], op=ALU.pow)
+            nc.gpsimd.tensor_scalar(out=nmean[s][:], in0=mv[s][:, :, 0], scalar1=-1.0, scalar2=1.0, op0=ALU.mult, op1=ALU.mult)
+
+        def ln_norm(s, k):
+            nc.gpsimd.tensor_scalar(out=xn[s][:, k, :].rearrange("p (t q) -> p t q", t=T), in0=x[s][:, k, :].rearrange("p (q t) -> p t q", t=T),
+                                    scalar1=nmean[s][:, k : k + 1], scalar2=rstd[s][:, k : k + 1], op0=ALU.add, op1=ALU.mult)
+
+        banks = {}
+
+        def ln_turn(s, k):
+            bank = ps_t.tile([P, T, P], F32, name="tr")
+            for j in range(T):
+                nc.tensor.transpose(bank[:, j, :], xn[s][:, k, j * P : (j + 1) * P], ident[:])
+            banks[(s, k)] = bank
+
+        def ln_gain(s, k):
+            nc.vector.tensor_tensor(out=mg[s][:, k * 512 : (k + 1) * 512].rearrange("p (r t) -> p r t", t=T), in0=banks[(s, k)][:].rearrange("p t r -> p r t"),
+                                    in1=gain[:].unsqueeze(1).to_broadcast([P, P, T]), op=ALU.mult)
+
+        def ln_quant(s):
+            quantize(mq[s][:], ms[s][:], mg[s][:])
+
+        def turn(src, dst, b):
+            words = src[:].bitcast(F32)
+            bank = ps_t.tile([P, 2, 2, P], F32, name="tr")
+            for i in range(2):
+                for u in range(2):
+                    w0 = 256 * (2 * b + i)
+                    nc.tensor.transpose(bank[:, i, u, :], words[:, w0 + u : w0 + 256 : 2], ident[:])
+            dv = dst[:, b * 1024 : (b + 1) * 1024].bitcast(F32).rearrange("p (i r u) -> p i r u", i=2, u=2)
+            nc.scalar.copy(out=dv, in_=bank[:].rearrange("p i u r -> p i r u"))
+
+        wv_w = sb([P, T, D], BF16, "wv_w")
+        wv_g = sb([P, D * T], BF16, "wv_g")
+        wv_q = sb([P, D], U32, "wv_q")
+        wv_s = sb([P, D], U8, "wv_s")
+        wg_g = sb([P, D * T], BF16, "wg_g")
+        wg_q = sb([P, D], U32, "wg_q")
+        wg_s = sb([P, D], U8, "wg_s")
+
+        def interleave(dst, src, k):
+            nc.gpsimd.tensor_scalar(
+                out=dst[:, k * 512 : (k + 1) * 512].rearrange("p (n t) -> p n t", t=T),
+                in0=src[:, :, k * P : (k + 1) * P].rearrange("p t n -> p n t"),
+                scalar1=1.0, scalar2=1.0, op0=ALU.mult, op1=ALU.mult)
+
+        def widen(k):
+            nc.scalar.activation(out=wv_w[:, k, :], in_=wv_bytes[:, k, :].bitcast(FP8), func=ACT.Copy, scale=sv[:, k : k + 1])
+
+        vb = [sb([P, T, D], BF16, "vb%d" % s) for s in range(S)]
+        vg = [sb([P, D * T], BF16, "vg%d" % s) for s in range(S)]
+        vq = [sb([P, D], U32, "vq%d" % s) for s in range(S)]
+        vs = [sb([P, D], U8, "vs%d" % s) for s in range(S)]
+        gt = [sb([P, T, D], F32, "gt%d" % s) for s in range(S)]
+
+        def project(dst, s, k, wq, ws):
+            cols = slice(k * P, (k + 1) * P)
+            nc.tensor.matmul_mx(out=dst, lhsT=mq[s][:, cols].bitcast(FP8X4), lhsT_scale=ms[s][:, cols],
+                                rhs=wq[:].bitcast(FP8X4), rhs_scale=ws[:], start=True, stop=True)
+
+        def values(s, k):
+            acc = ps_m.tile([P, D], F32, name="mm")
+            project(acc[:], s, k, wv_q, wv_s)
+            nc.scalar.activation(out=vb[s][:, k, :], in_=acc[:], func=ACT.Copy, scale=th[:, s, k : k + 1])
+
+        def gate(s, k):
+            acc = ps_m.tile([P, D], F32, name="mm")
+            project(acc[:], s, k, wg_q, wg_s)
+            nc.scalar.activation(out=gt[s][:, k, :], in_=acc[:], func=ACT.Tanh, scale=0.5)
+
+        nm = [sb([P, H], F32, "nm%d" % i) for i in range(T)]
+        sums = [sb([P, H], F32, "sums%d" % i) for i in range(T)]
+        rs = [sb([P, H], F32, "rs%d" % i) for i in range(T)]
+        ez = [sb([P, H, R], F32, "ez%d" % i) for i in range(T)]
+        ab = [sb([P, H * R], BF16, "ab%d" % i) for i in range(T)]
+        ag = [sb([P, H * P * T], BF16, "ag%d" % i) for i in range(T)]
+        aq = [sb([P, H * P], U32, "aq%d" % i) for i in range(T)]
+        asc = [sb([P, H * P], U8, "as%d" % i) for i in range(T)]
+        osb = [[sb([P, D], F32, "o%d_%d" % (i, s)) for s in range(S)] for i in range(T)]
+
+        def row_max(i):
+            tiles = [zt[i]] + [sb([P, H, R >> n], BF16, "f%d_%d" % (i, n)) for n in range(1, 5)]
+
+            def fold(n):
+                w = R >> n
+                return lambda: nc.vector.tensor_tensor(out=tiles[n][:], in0=tiles[n - 1][:, :, 0:w], in1=tiles[n - 1][:, :, w : 2 * w], op=ALU.max)
+
+            return [fold(n) for n in range(1, 5)] + [lambda: nc.vector.tensor_reduce(out=nm[i][:], in_=tiles[4][:], axis=AX.X, op=ALU.max, negate=True)]
+
+        def exps(i, h):
+            nc.scalar.activation(out=ez[i][:, h, :], in_=zt[i][:, h, :], func=ACT.Exp, bias=nm[i][:, h : h + 1], scale=1.0, accum_out=sums[i][:, h : h + 1])
+
+        def recip(i):
+            nc.vector.reciprocal(out=rs[i][:], in_=sums[i][:])
+
+        def weights(i, h):
+            nc.vector.scalar_tensor_tensor(out=ab[i][:, h * R : (h + 1) * R], in0=ez[i][:, h, :], scalar=rs[i][:, h : h + 1], in1=cb[h // 2][:, h % 2, :], op0=ALU.mult, op1=ALU.mult)
+
+        def a_quant(i):
+            quantize(aq[i][:], asc[i][:], ag[i][:])
+
+        def average(i, s):
+            acc = ps_m.tile([P, D], F32, name="mm")
+            for h in range(H):
+                cols = slice(h * P, (h + 1) * P)
+                nc.tensor.matmul_mx(out=acc[:, cols], lhsT=aq[i][:, cols].bitcast(FP8X4), lhsT_scale=asc[i][:, cols],
+                                    rhs=vq[s][:, cols].bitcast(FP8X4), rhs_scale=vs[s][:, cols], start=True, stop=True)
+            nc.vector.scalar_tensor_tensor(out=osb[i][s][:], in0=gt[s][:, i, :], scalar=1.0, in1=acc[:], op0=ALU.add, op1=ALU.mult)
+            nc.sync.dma_start(out=out[s].rearrange("(p t) f -> p t f", t=T)[:, i, :], in_=osb[i][s][:])
+
+        ctx.enter_context(tc.manual_schedule())
+
+        def v_gain(s):
+            return [lambda k=k: (ln_turn(s, k), ln_gain(s, k)) for k in range(T)]
+
+        def v_weights(i):
+            return [lambda: recip(i)] + [lambda h=h: weights(i, h) for h in range(H)]
+
+        run(ln_stats(0))
+        ln_scales(0)
+        for k in range(T):
+            widen(k)
+        for k in range(T):
+            ln_norm(0, k)
+        weave(row_max(0), ln_stats(1))
+        for h in range(H):
+            exps(0, h)
+        ln_scales(1)
+        for h in range(H):
+            spread(h)
+        for k in range(T):
+            interleave(wv_g, wv_w, k)
+        for k in range(T):
+            ln_norm(1, k)
+        weave(row_max(1), v_gain(0))
+        for h in range(H):
+            exps(1, h)
+        weave(row_max(2), row_max(3))
+        for i in range(2, T):
+            for h in range(H):
+                exps(i, h)
+        ln_quant(0)
+        quantize(wv_q[:], wv_s[:], wv_g[:])
+        nc.vector.tensor_scalar(out=th[:], in0=tv[:], scalar1=0.5, scalar2=None, op0=ALU.mult)
+        for k in range(T):
+            interleave(wg_g, wg_raw, k)
+        weave(v_weights(0), v_gain(1))
+        for k in range(T):
+            values(0, k)
+        for k in range(T):
+            interleave(vg[0], vb[0], k)
+        ln_quant(1)
+        run(v_weights(1))
+        for k in range(T):
+            values(1, k)
+        for k in range(T):
+            interleave(vg[1], vb[1], k)
+        for b in range(2):
+            turn(ab[0], ag[0], b)
+        quantize(wg_q[:], wg_s[:], wg_g[:])
+        run(v_weights(2))
+        for k in range(2):
+            gate(0, k)
+        for b in range(2):
+            turn(ab[1], ag[1], b)
+        quantize(vq[0][:], vs[0][:], vg[0][:])
+        a_quant(0)
+        run(v_weights(3))
+        for k in range(2):
+            gate(1, k)
+        for b in range(2):
+            turn(ab[2], ag[2], b)
+        a_quant(1)
+        quantize(vq[1][:], vs[1][:], vg[1][:])
+        for b in range(2):
+            turn(ab[3], ag[3], b)
+        average(0, 0)
+        average(1, 0)
+        for k in range(2, T):
+            gate(0, k)
+        average(0, 1)
+        a_quant(2)
+        average(1, 1)
+        for k in range(2, T):
+            gate(1, k)
+        a_quant(3)
+        for i in range(2, T):
+            average(i, 0)
+        for i in range(2, T):
+            average(i, 1)

@@ -50,19 +50,24 @@ def tile_msapairweightedaveraging_kernel(tc, m, ln_g, w_v_bytes, w_v_scale, w_g,
         nc.vector.memset(cst[:], 0.0)
         mv_ = [m[s].rearrange("(p t) f -> p t f", t=T) for s in range(S)]
         zv = z.rearrange("h (p t) j -> t p h j", t=T)
-        for k in range(2):
-            nc.sync.dma_start(out=x[0][:, 2 * k : 2 * k + 2, :], in_=mv_[0][:, 2 * k : 2 * k + 2, :])
         nc.scalar.dma_start(out=cst[0:4, :], in_=c)
         nc.scalar.dma_start(out=sv[:], in_=w_v_scale.rearrange("(p t) o -> p (t o)", t=T))
         nc.scalar.dma_start(out=gain[:], in_=ln_g.rearrange("(p t) -> p t", t=T))
         nc.scalar.dma_start(out=tv[:], in_=t.rearrange("s (p t) -> p s t", t=T))
+        nc.scalar.dma_start(out=sv[:], in_=w_v_scale.rearrange("(p t) o -> p (t o)", t=T))
+        nc.scalar.dma_start(out=gain[:], in_=ln_g.rearrange("(p t) -> p t", t=T))
+        nc.scalar.dma_start(out=cst[0:4, :], in_=c)
+        nc.scalar.dma_start(out=tv[:], in_=t.rearrange("s (p t) -> p s t", t=T))
+        for k in range(2):
+            nc.sync.dma_start(out=x[0][:, 2 * k : 2 * k + 2, :], in_=mv_[0][:, 2 * k : 2 * k + 2, :])
+        nc.sync.dma_start(out=wv_bytes[:], in_=w_v_bytes.rearrange("(p t) n -> p t n", t=T))
         nc.sync.dma_start(out=zt[0][:], in_=zv[0])
         nc.sync.dma_start(out=x[1][:], in_=mv_[1])
         nc.sync.dma_start(out=zt[1][:], in_=zv[1])
-        nc.sync.dma_start(out=wv_bytes[:], in_=w_v_bytes.rearrange("(p t) n -> p t n", t=T))
         nc.sync.dma_start(out=zt[2][:], in_=zv[2])
         nc.sync.dma_start(out=wg_raw[:], in_=w_g.rearrange("(p t) n -> p t n", t=T))
         nc.sync.dma_start(out=zt[3][:], in_=zv[3])
+        nc.sync.dma_start(out=wg_raw[:], in_=w_g.rearrange("(p t) n -> p t n", t=T))
 
         warm = sb([P, 1], F32, "warm")
         nc.vector.memset(warm[:], 0.0)
@@ -114,14 +119,32 @@ def tile_msapairweightedaveraging_kernel(tc, m, ln_g, w_v_bytes, w_v_scale, w_g,
 
             return [bn(k) for k in range(T)] + [agg(k) for k in range(T)]
 
+        junk = sb([P, T, D], BF16, "junk")
+        tot = sb([P, T], F32, "tot")
+        ssq = sb([P, T], F32, "ssq")
+
+        def ln_stats_scalar(s):
+            for k in range(T):
+                nc.scalar.activation(out=junk[:, k, :], in_=x[s][:, k, :], func=ACT.Copy, scale=1.0, accum_out=tot[:, k : k + 1])
+            nc.gpsimd.tensor_scalar(out=nmean[s][:], in0=tot[:], scalar1=-1.0 / D, scalar2=1.0, op0=ALU.mult, op1=ALU.mult)
+            for k in range(T):
+                nc.scalar.activation(out=junk[:, k, :], in_=x[s][:, k, :], func=ACT.Square, scale=1.0, bias=nmean[s][:, k : k + 1], accum_out=ssq[:, k : k + 1])
+            nc.gpsimd.tensor_scalar(out=ve[s][:], in0=ssq[:], scalar1=1.0 / D, scalar2=EPS, op0=ALU.mult, op1=ALU.add)
+            nc.gpsimd.tensor_tensor(out=rstd[s][:], in0=ve[s][:], in1=mhalf[:], op=ALU.pow)
+
         def ln_scales(s):
             nc.gpsimd.tensor_scalar(out=ve[s][:], in0=mv[s][:, :, 1], scalar1=1.0, scalar2=EPS, op0=ALU.mult, op1=ALU.add)
             nc.gpsimd.tensor_tensor(out=rstd[s][:], in0=ve[s][:], in1=mhalf[:], op=ALU.pow)
             nc.gpsimd.tensor_scalar(out=nmean[s][:], in0=mv[s][:, :, 0], scalar1=-1.0, scalar2=1.0, op0=ALU.mult, op1=ALU.mult)
 
+        nmr = [sb([P, T], F32, "nmr%d" % s) for s in range(S)]
+
+        def ln_bias(s):
+            nc.gpsimd.tensor_tensor(out=nmr[s][:], in0=nmean[s][:], in1=rstd[s][:], op=ALU.mult)
+
         def ln_norm(s, k):
-            nc.gpsimd.tensor_scalar(out=xn[s][:, k, :].rearrange("p (t q) -> p t q", t=T), in0=x[s][:, k, :].rearrange("p (q t) -> p t q", t=T),
-                                    scalar1=nmean[s][:, k : k + 1], scalar2=rstd[s][:, k : k + 1], op0=ALU.add, op1=ALU.mult)
+            nc.scalar.activation(out=xn[s][:, k, :].rearrange("p (t q) -> p t q", t=T), in_=x[s][:, k, :].rearrange("p (q t) -> p t q", t=T),
+                                 func=ACT.Identity, scale=rstd[s][:, k : k + 1], bias=nmr[s][:, k : k + 1])
 
         banks = {}
 
@@ -156,16 +179,19 @@ def tile_msapairweightedaveraging_kernel(tc, m, ln_g, w_v_bytes, w_v_scale, w_g,
         wg_q = sb([P, D], U32, "wg_q")
         wg_s = sb([P, D], U8, "wg_s")
 
-        def interleave(dst, src, k):
-            nc.gpsimd.tensor_scalar(
-                out=dst[:, k * 512 : (k + 1) * 512].rearrange("p (n t) -> p n t", t=T),
-                in0=src[:, :, k * P : (k + 1) * P].rearrange("p t n -> p n t"),
-                scalar1=1.0, scalar2=1.0, op0=ALU.mult, op1=ALU.mult)
+        def inter_g(dst, src, k):
+            nc.gpsimd.tensor_scalar(out=dst[:, k * 512 : (k + 1) * 512].rearrange("p (n t) -> p n t", t=T), in0=src[:, :, k * P : (k + 1) * P].rearrange("p t n -> p n t"),
+                                    scalar1=1.0, scalar2=1.0, op0=ALU.mult, op1=ALU.mult)
+
+        def inter_s(dst, src, k):
+            nc.scalar.copy(out=dst[:, k * 512 : (k + 1) * 512].rearrange("p (n t) -> p n t", t=T), in_=src[:, :, k * P : (k + 1) * P].rearrange("p t n -> p n t"))
+
+        def inter_v(dst, src, k):
+            nc.vector.tensor_copy(out=dst[:, k * 512 : (k + 1) * 512].rearrange("p (n t) -> p n t", t=T), in_=src[:, :, k * P : (k + 1) * P].rearrange("p t n -> p n t"))
 
         def widen(k):
             nc.scalar.activation(out=wv_w[:, k, :], in_=wv_bytes[:, k, :].bitcast(FP8), func=ACT.Copy, scale=sv[:, k : k + 1])
 
-        vb = [sb([P, T, D], BF16, "vb%d" % s) for s in range(S)]
         vg = [sb([P, D * T], BF16, "vg%d" % s) for s in range(S)]
         vq = [sb([P, D], U32, "vq%d" % s) for s in range(S)]
         vs = [sb([P, D], U8, "vs%d" % s) for s in range(S)]
@@ -175,6 +201,8 @@ def tile_msapairweightedaveraging_kernel(tc, m, ln_g, w_v_bytes, w_v_scale, w_g,
             cols = slice(k * P, (k + 1) * P)
             nc.tensor.matmul_mx(out=dst, lhsT=mq[s][:, cols].bitcast(FP8X4), lhsT_scale=ms[s][:, cols],
                                 rhs=wq[:].bitcast(FP8X4), rhs_scale=ws[:], start=True, stop=True)
+
+        vb = [sb([P, T, D], BF16, "vb%d" % s) for s in range(S)]
 
         def values(s, k):
             acc = ps_m.tile([P, D], F32, name="mm")
@@ -196,14 +224,10 @@ def tile_msapairweightedaveraging_kernel(tc, m, ln_g, w_v_bytes, w_v_scale, w_g,
         asc = [sb([P, H * P], U8, "as%d" % i) for i in range(T)]
         osb = [[sb([P, D], F32, "o%d_%d" % (i, s)) for s in range(S)] for i in range(T)]
 
+        zneg = sb([P, H, R], BF16, "zneg")
+
         def row_max(i):
-            tiles = [zt[i]] + [sb([P, H, R >> n], BF16, "f%d_%d" % (i, n)) for n in range(1, 5)]
-
-            def fold(n):
-                w = R >> n
-                return lambda: nc.vector.tensor_tensor(out=tiles[n][:], in0=tiles[n - 1][:, :, 0:w], in1=tiles[n - 1][:, :, w : 2 * w], op=ALU.max)
-
-            return [fold(n) for n in range(1, 5)] + [lambda: nc.vector.tensor_reduce(out=nm[i][:], in_=tiles[4][:], axis=AX.X, op=ALU.max, negate=True)]
+            return [lambda h=h: nc.vector.tensor_scalar(out=zneg[:, h, :], in0=zt[i][:, h, :], scalar1=-1.0, scalar2=None, op0=ALU.mult, op1=ALU.min, accum_out=nm[i][:, h : h + 1]) for h in range(H)]
 
         def exps(i, h):
             nc.scalar.activation(out=ez[i][:, h, :], in_=zt[i][:, h, :], func=ACT.Exp, bias=nm[i][:, h : h + 1], scale=1.0, accum_out=sums[i][:, h : h + 1])
@@ -234,75 +258,74 @@ def tile_msapairweightedaveraging_kernel(tc, m, ln_g, w_v_bytes, w_v_scale, w_g,
         def v_weights(i):
             return [lambda: recip(i)] + [lambda h=h: weights(i, h) for h in range(H)]
 
-        run(ln_stats(0))
-        ln_scales(0)
-        for k in range(T):
-            widen(k)
-        for k in range(T):
-            ln_norm(0, k)
-        weave(row_max(0), ln_stats(1))
-        for h in range(H):
-            exps(0, h)
-        ln_scales(1)
-        for h in range(H):
-            spread(h)
-        for k in range(T):
-            interleave(wv_g, wv_w, k)
-        for k in range(T):
-            ln_norm(1, k)
-        weave(row_max(1), v_gain(0))
-        for h in range(H):
-            exps(1, h)
-        weave(row_max(2), row_max(3))
-        for i in range(2, T):
+        def all_exps(i):
             for h in range(H):
                 exps(i, h)
-        ln_quant(0)
-        quantize(wv_q[:], wv_s[:], wv_g[:])
+
+        def each(f, *a):
+            for k in range(T):
+                f(*a, k)
+
+        run(ln_stats(0))
+        ln_scales(0)
+        ln_bias(0)
+        each(widen)
+        run(row_max(0))
+        all_exps(0)
+        weave(ln_stats(1), row_max(1))
+        ln_scales(1)
+        ln_bias(1)
+        each(ln_norm, 0)
+        for h in range(H):
+            spread(h)
+        run(row_max(2))
+        all_exps(1)
+        each(inter_g, wv_g, wv_w)
+        weave(v_gain(0), v_weights(0))
         nc.vector.tensor_scalar(out=th[:], in0=tv[:], scalar1=0.5, scalar2=None, op0=ALU.mult)
-        for k in range(T):
-            interleave(wg_g, wg_raw, k)
-        weave(v_weights(0), v_gain(1))
-        for k in range(T):
-            values(0, k)
-        for k in range(T):
-            interleave(vg[0], vb[0], k)
-        ln_quant(1)
-        run(v_weights(1))
-        for k in range(T):
-            values(1, k)
-        for k in range(T):
-            interleave(vg[1], vb[1], k)
+        each(ln_norm, 1)
+        run(row_max(3))
+        ln_quant(0)
         for b in range(2):
             turn(ab[0], ag[0], b)
-        quantize(wg_q[:], wg_s[:], wg_g[:])
+        all_exps(2)
+        quantize(wv_q[:], wv_s[:], wv_g[:])
+        weave(v_gain(1), v_weights(1))
+        each(inter_g, wg_g, wg_raw)
+        each(values, 0)
+        all_exps(3)
+        ln_quant(1)
+        each(inter_g, vg[0], vb[0])
         run(v_weights(2))
-        for k in range(2):
-            gate(0, k)
+        quantize(wg_q[:], wg_s[:], wg_g[:])
+        a_quant(0)
+        each(values, 1)
+        each(inter_g, vg[1], vb[1])
         for b in range(2):
             turn(ab[1], ag[1], b)
-        quantize(vq[0][:], vs[0][:], vg[0][:])
-        a_quant(0)
+        gate(0, 0)
+        gate(1, 0)
         run(v_weights(3))
-        for k in range(2):
-            gate(1, k)
+        quantize(vq[0][:], vs[0][:], vg[0][:])
+        a_quant(1)
+        gate(0, 1)
+        gate(1, 1)
         for b in range(2):
             turn(ab[2], ag[2], b)
-        a_quant(1)
+        average(0, 0)
         quantize(vq[1][:], vs[1][:], vg[1][:])
+        a_quant(2)
         for b in range(2):
             turn(ab[3], ag[3], b)
-        average(0, 0)
         average(1, 0)
-        for k in range(2, T):
-            gate(0, k)
         average(0, 1)
-        a_quant(2)
+        gate(0, 2)
+        gate(1, 2)
         average(1, 1)
-        for k in range(2, T):
-            gate(1, k)
         a_quant(3)
-        for i in range(2, T):
-            average(i, 0)
-        for i in range(2, T):
-            average(i, 1)
+        gate(0, 3)
+        gate(1, 3)
+        average(2, 0)
+        average(2, 1)
+        average(3, 0)
+        average(3, 1)

@@ -50,24 +50,19 @@ def tile_msapairweightedaveraging_kernel(tc, m, ln_g, w_v_bytes, w_v_scale, w_g,
         nc.vector.memset(cst[:], 0.0)
         mv_ = [m[s].rearrange("(p t) f -> p t f", t=T) for s in range(S)]
         zv = z.rearrange("h (p t) j -> t p h j", t=T)
-        nc.scalar.dma_start(out=cst[0:4, :], in_=c)
-        nc.scalar.dma_start(out=sv[:], in_=w_v_scale.rearrange("(p t) o -> p (t o)", t=T))
-        nc.scalar.dma_start(out=gain[:], in_=ln_g.rearrange("(p t) -> p t", t=T))
-        nc.scalar.dma_start(out=tv[:], in_=t.rearrange("s (p t) -> p s t", t=T))
         nc.scalar.dma_start(out=sv[:], in_=w_v_scale.rearrange("(p t) o -> p (t o)", t=T))
         nc.scalar.dma_start(out=gain[:], in_=ln_g.rearrange("(p t) -> p t", t=T))
         nc.scalar.dma_start(out=cst[0:4, :], in_=c)
         nc.scalar.dma_start(out=tv[:], in_=t.rearrange("s (p t) -> p s t", t=T))
         for k in range(2):
             nc.sync.dma_start(out=x[0][:, 2 * k : 2 * k + 2, :], in_=mv_[0][:, 2 * k : 2 * k + 2, :])
-        nc.sync.dma_start(out=wv_bytes[:], in_=w_v_bytes.rearrange("(p t) n -> p t n", t=T))
         nc.sync.dma_start(out=zt[0][:], in_=zv[0])
+        nc.sync.dma_start(out=wv_bytes[:], in_=w_v_bytes.rearrange("(p t) n -> p t n", t=T))
         nc.sync.dma_start(out=x[1][:], in_=mv_[1])
+        nc.sync.dma_start(out=wg_raw[:], in_=w_g.rearrange("(p t) n -> p t n", t=T))
         nc.sync.dma_start(out=zt[1][:], in_=zv[1])
         nc.sync.dma_start(out=zt[2][:], in_=zv[2])
-        nc.sync.dma_start(out=wg_raw[:], in_=w_g.rearrange("(p t) n -> p t n", t=T))
         nc.sync.dma_start(out=zt[3][:], in_=zv[3])
-        nc.sync.dma_start(out=wg_raw[:], in_=w_g.rearrange("(p t) n -> p t n", t=T))
 
         warm = sb([P, 1], F32, "warm")
         nc.vector.memset(warm[:], 0.0)
@@ -76,6 +71,8 @@ def tile_msapairweightedaveraging_kernel(tc, m, ln_g, w_v_bytes, w_v_scale, w_g,
         make_identity(nc, ident[:])
         mhalf = sb([P, T], F32, "mhalf")
         nc.gpsimd.memset(mhalf[:], -0.5)
+        csp = sb([P, D], BF16, "csp")
+        nc.gpsimd.tensor_scalar(out=csp[:].rearrange("p (u q e) -> p u q e", u=2, e=2), in0=cst[:].rearrange("p (q u e) -> p u q e", u=2, e=2), scalar1=1.0, scalar2=1.0, op0=ALU.mult, op1=ALU.mult)
         sel = sb([P, 8], BF16, "sel")
         nc.vector.tensor_copy(out=sel[:], in_=ident[:, 0:8])
         th = sb([P, S, T], F32, "th")
@@ -95,7 +92,7 @@ def tile_msapairweightedaveraging_kernel(tc, m, ln_g, w_v_bytes, w_v_scale, w_g,
                     step()
 
         def spread(h):
-            nc.tensor.matmul(cb[h // 2][:, h % 2, :], lhsT=sel[:, h : h + 1].to_broadcast([P, P]), rhs=cst[:], start=True, stop=True)
+            nc.tensor.matmul(cb[h // 2][:, h % 2, :], lhsT=sel[:, h : h + 1].to_broadcast([P, P]), rhs=csp[:], start=True, stop=True)
 
         def quantize(codes, scales, src):
             nc.vector.quantize_mx(out=codes.bitcast(FP8X4), scales=scales, in_=src)
@@ -119,18 +116,24 @@ def tile_msapairweightedaveraging_kernel(tc, m, ln_g, w_v_bytes, w_v_scale, w_g,
 
             return [bn(k) for k in range(T)] + [agg(k) for k in range(T)]
 
-        junk = sb([P, T, D], BF16, "junk")
-        tot = sb([P, T], F32, "tot")
-        ssq = sb([P, T], F32, "ssq")
+        junk = sb([P, 2, D], BF16, "junk")
+        tot = sb([P, 2], F32, "tot")
+        ssq = sb([P, 2], F32, "ssq")
 
-        def ln_stats_scalar(s):
-            for k in range(T):
-                nc.scalar.activation(out=junk[:, k, :], in_=x[s][:, k, :], func=ACT.Copy, scale=1.0, accum_out=tot[:, k : k + 1])
-            nc.gpsimd.tensor_scalar(out=nmean[s][:], in0=tot[:], scalar1=-1.0 / D, scalar2=1.0, op0=ALU.mult, op1=ALU.mult)
-            for k in range(T):
-                nc.scalar.activation(out=junk[:, k, :], in_=x[s][:, k, :], func=ACT.Square, scale=1.0, bias=nmean[s][:, k : k + 1], accum_out=ssq[:, k : k + 1])
-            nc.gpsimd.tensor_scalar(out=ve[s][:], in0=ssq[:], scalar1=1.0 / D, scalar2=EPS, op0=ALU.mult, op1=ALU.add)
-            nc.gpsimd.tensor_tensor(out=rstd[s][:], in0=ve[s][:], in1=mhalf[:], op=ALU.pow)
+        def sum_s(k):
+            nc.scalar.activation(out=junk[:, k - 2, :], in_=x[0][:, k, :], func=ACT.Copy, scale=1.0, accum_out=tot[:, k - 2 : k - 1])
+
+        def mean_s():
+            nc.gpsimd.tensor_scalar(out=nmean[0][:, 2:4], in0=tot[:], scalar1=-1.0 / D, scalar2=1.0, op0=ALU.mult, op1=ALU.mult)
+
+        def square_s(k):
+            nc.scalar.activation(out=junk[:, k - 2, :], in_=x[0][:, k, :], func=ACT.Square, scale=1.0, bias=nmean[0][:, k : k + 1], accum_out=ssq[:, k - 2 : k - 1])
+
+        def ln_scales0():
+            nc.gpsimd.tensor_scalar(out=nmean[0][:, 0:2], in0=mv[0][:, 0:2, 0], scalar1=-1.0, scalar2=1.0, op0=ALU.mult, op1=ALU.mult)
+            nc.gpsimd.tensor_scalar(out=ve[0][:, 0:2], in0=mv[0][:, 0:2, 1], scalar1=1.0, scalar2=EPS, op0=ALU.mult, op1=ALU.add)
+            nc.gpsimd.tensor_scalar(out=ve[0][:, 2:4], in0=ssq[:], scalar1=1.0 / D, scalar2=EPS, op0=ALU.mult, op1=ALU.add)
+            nc.gpsimd.tensor_tensor(out=rstd[0][:], in0=ve[0][:], in1=mhalf[:], op=ALU.pow)
 
         def ln_scales(s):
             nc.gpsimd.tensor_scalar(out=ve[s][:], in0=mv[s][:, :, 1], scalar1=1.0, scalar2=EPS, op0=ALU.mult, op1=ALU.add)
@@ -167,7 +170,7 @@ def tile_msapairweightedaveraging_kernel(tc, m, ln_g, w_v_bytes, w_v_scale, w_g,
             for i in range(2):
                 for u in range(2):
                     w0 = 256 * (2 * b + i)
-                    nc.tensor.transpose(bank[:, i, u, :], words[:, w0 + u : w0 + 256 : 2], ident[:])
+                    nc.tensor.transpose(bank[:, i, u, :], words[:, w0 + P * u : w0 + P * (u + 1)], ident[:])
             dv = dst[:, b * 1024 : (b + 1) * 1024].bitcast(F32).rearrange("p (i r u) -> p i r u", i=2, u=2)
             nc.scalar.copy(out=dv, in_=bank[:].rearrange("p i u r -> p i r u"))
 
@@ -230,7 +233,7 @@ def tile_msapairweightedaveraging_kernel(tc, m, ln_g, w_v_bytes, w_v_scale, w_g,
             return [lambda h=h: nc.vector.tensor_scalar(out=zneg[:, h, :], in0=zt[i][:, h, :], scalar1=-1.0, scalar2=None, op0=ALU.mult, op1=ALU.min, accum_out=nm[i][:, h : h + 1]) for h in range(H)]
 
         def exps(i, h):
-            nc.scalar.activation(out=ez[i][:, h, :], in_=zt[i][:, h, :], func=ACT.Exp, bias=nm[i][:, h : h + 1], scale=1.0, accum_out=sums[i][:, h : h + 1])
+            nc.scalar.activation(out=ez[i][:, h, :].rearrange("p (u q e) -> p u q e", u=2, e=2), in_=zt[i][:, h, :].rearrange("p (q u e) -> p u q e", u=2, e=2), func=ACT.Exp, bias=nm[i][:, h : h + 1], scale=1.0, accum_out=sums[i][:, h : h + 1])
 
         def recip(i):
             nc.vector.reciprocal(out=rs[i][:], in_=sums[i][:])
@@ -250,82 +253,99 @@ def tile_msapairweightedaveraging_kernel(tc, m, ln_g, w_v_bytes, w_v_scale, w_g,
             nc.vector.scalar_tensor_tensor(out=osb[i][s][:], in0=gt[s][:, i, :], scalar=1.0, in1=acc[:], op0=ALU.add, op1=ALU.mult)
             nc.sync.dma_start(out=out[s].rearrange("(p t) f -> p t f", t=T)[:, i, :], in_=osb[i][s][:])
 
+        def halve_t():
+            nc.vector.tensor_scalar(out=th[:], in0=tv[:], scalar1=0.5, scalar2=None, op0=ALU.mult)
+
         ctx.enter_context(tc.manual_schedule())
-
-        def v_gain(s):
-            return [lambda k=k: (ln_turn(s, k), ln_gain(s, k)) for k in range(T)]
-
-        def v_weights(i):
-            return [lambda: recip(i)] + [lambda h=h: weights(i, h) for h in range(H)]
-
-        def all_exps(i):
-            for h in range(H):
-                exps(i, h)
-
-        def each(f, *a):
-            for k in range(T):
-                f(*a, k)
-
-        run(ln_stats(0))
-        ln_scales(0)
-        ln_bias(0)
-        each(widen)
+        run(ln_stats(0)[0:2] + ln_stats(0)[4:6])
+        sum_s(2); sum_s(3); mean_s()
+        spread(0); spread(1); spread(2); spread(3)
         run(row_max(0))
-        all_exps(0)
-        weave(ln_stats(1), row_max(1))
-        ln_scales(1)
-        ln_bias(1)
-        each(ln_norm, 0)
-        for h in range(H):
-            spread(h)
+        run(ln_stats(1))
+        square_s(2); square_s(3)
+        exps(0, 0); exps(0, 1)
+        run(row_max(1))
+        exps(0, 2); exps(0, 3)
+        ln_scales0(); ln_bias(0)
+        ln_norm(0, 2); ln_norm(0, 3)
+        recip(0)
+        halve_t()
+        widen(2); widen(3)
+        ln_scales(1); ln_bias(1)
+        ln_norm(0, 0); ln_norm(0, 1)
+        ln_norm(1, 0); ln_norm(1, 1)
+        widen(0); widen(1)
+        ln_turn(0, 2); ln_gain(0, 2)
+        ln_turn(0, 3); ln_gain(0, 3)
+        ln_norm(1, 2); ln_norm(1, 3)
+        weights(0, 0); weights(0, 1)
+        ln_turn(0, 0); ln_gain(0, 0)
+        ln_turn(0, 1); ln_gain(0, 1)
+        exps(1, 2); exps(1, 3)
+        exps(1, 0); exps(1, 1)
         run(row_max(2))
-        all_exps(1)
-        each(inter_g, wv_g, wv_w)
-        weave(v_gain(0), v_weights(0))
-        nc.vector.tensor_scalar(out=th[:], in0=tv[:], scalar1=0.5, scalar2=None, op0=ALU.mult)
-        each(ln_norm, 1)
-        run(row_max(3))
+        ln_turn(1, 1); ln_gain(1, 1)
+        weights(0, 2); weights(0, 3)
+        ln_turn(1, 3); ln_gain(1, 3)
+        ln_turn(1, 0); ln_gain(1, 0)
+        ln_turn(1, 2); ln_gain(1, 2)
+        inter_g(wg_g, wg_raw, 0); inter_g(wg_g, wg_raw, 1); inter_g(wg_g, wg_raw, 2); inter_g(wg_g, wg_raw, 3)
         ln_quant(0)
-        for b in range(2):
-            turn(ab[0], ag[0], b)
-        all_exps(2)
+        inter_g(wv_g, wv_w, 0); inter_g(wv_g, wv_w, 1); inter_g(wv_g, wv_w, 2); inter_g(wv_g, wv_w, 3)
+        exps(2, 2); exps(2, 3)
         quantize(wv_q[:], wv_s[:], wv_g[:])
-        weave(v_gain(1), v_weights(1))
-        each(inter_g, wg_g, wg_raw)
-        each(values, 0)
-        all_exps(3)
+        turn(ab[0], ag[0], 0)
+        exps(2, 0); exps(2, 1)
+        values(0, 3)
+        turn(ab[0], ag[0], 1)
         ln_quant(1)
-        each(inter_g, vg[0], vb[0])
-        run(v_weights(2))
-        quantize(wg_q[:], wg_s[:], wg_g[:])
+        values(0, 1)
+        run(row_max(3))
+        values(0, 2)
+        recip(1)
+        recip(2)
+        weights(1, 0); weights(1, 1)
+        values(0, 0)
         a_quant(0)
-        each(values, 1)
-        each(inter_g, vg[1], vb[1])
-        for b in range(2):
-            turn(ab[1], ag[1], b)
-        gate(0, 0)
-        gate(1, 0)
-        run(v_weights(3))
+        exps(3, 0); exps(3, 1)
+        quantize(wg_q[:], wg_s[:], wg_g[:])
+        weights(1, 2); weights(1, 3)
+        exps(3, 2); exps(3, 3)
+        inter_g(vg[0], vb[0], 0); inter_g(vg[0], vb[0], 1); inter_g(vg[0], vb[0], 2); inter_g(vg[0], vb[0], 3)
+        weights(2, 2); weights(2, 3)
+        recip(3)
+        values(1, 1)
+        turn(ab[1], ag[1], 0)
+        values(1, 3)
+        weights(2, 0); weights(2, 1)
+        turn(ab[1], ag[1], 1)
+        values(1, 0)
+        values(1, 2)
+        inter_g(vg[1], vb[1], 0); inter_g(vg[1], vb[1], 1); inter_g(vg[1], vb[1], 2); inter_g(vg[1], vb[1], 3)
+        gate(0, 1)
         quantize(vq[0][:], vs[0][:], vg[0][:])
         a_quant(1)
-        gate(0, 1)
-        gate(1, 1)
-        for b in range(2):
-            turn(ab[2], ag[2], b)
-        average(0, 0)
-        quantize(vq[1][:], vs[1][:], vg[1][:])
-        a_quant(2)
-        for b in range(2):
-            turn(ab[3], ag[3], b)
-        average(1, 0)
-        average(0, 1)
-        gate(0, 2)
+        turn(ab[2], ag[2], 0)
+        gate(0, 0)
+        turn(ab[2], ag[2], 1)
         gate(1, 2)
-        average(1, 1)
-        a_quant(3)
-        gate(0, 3)
+        weights(3, 0); weights(3, 1)
+        weights(3, 2); weights(3, 3)
+        average(1, 0)
+        gate(0, 2)
+        turn(ab[3], ag[3], 0)
+        average(0, 0)
+        a_quant(2)
+        quantize(vq[1][:], vs[1][:], vg[1][:])
+        turn(ab[3], ag[3], 1)
+        gate(1, 0)
         gate(1, 3)
+        gate(0, 3)
+        a_quant(3)
         average(2, 0)
         average(2, 1)
-        average(3, 0)
         average(3, 1)
+        average(0, 1)
+        gate(1, 1)
+        average(3, 0)
+        average(1, 1)

from contextlib import ExitStack

import concourse.mybir as mybir
from concourse.masks import make_identity

F32 = mybir.dt.float32
BF16 = mybir.dt.bfloat16
U32 = mybir.dt.uint32
U8 = mybir.dt.uint8
FP8 = mybir.dt.float8_e4m3fn
FP8X4 = mybir.dt.float8_e4m3fn_x4
ACT = mybir.ActivationFunctionType
ALU = mybir.AluOpType
AX = mybir.AxisListType

P = 128
S = 2
R = 512
H = 4
E = 128
D = H * E
T = 4
EPS = 1e-5

FLOPS = 2 * 2 * S * R * D * D + 2 * H * R * R * S * E


def tile_msapairweightedaveraging_kernel(tc, m, ln_g, w_v_bytes, w_v_scale, w_g, t, z, c, out):
    nc = tc.nc

    with ExitStack() as ctx:
        keep = ctx.enter_context(tc.tile_pool(name="keep", bufs=1))
        ps_c = ctx.enter_context(tc.psum_pool(name="ps_c", bufs=1))
        ps_t = ctx.enter_context(tc.psum_pool(name="ps_t", bufs=2))
        ps_m = ctx.enter_context(tc.psum_pool(name="ps_m", bufs=4))

        def sb(shape, dtype, name):
            return keep.tile(shape, dtype, name=name, align_bytes=64)


        x = [sb([P, T, D], BF16, "x%d" % s) for s in range(S)]
        zt = [sb([P, H, R], BF16, "z%d" % i) for i in range(T)]
        wg_raw = sb([P, T, D], BF16, "wg_raw")
        wv_bytes = sb([P, T, D], U8, "wv_bytes")
        cst = sb([P, D], BF16, "cst")
        sv = sb([P, T], F32, "sv")
        tv = sb([P, S, T], BF16, "tv")
        gain = sb([P, T], BF16, "gain")

        nc.vector.memset(cst[:], 0.0)
        mv_ = [m[s].rearrange("(p t) f -> p t f", t=T) for s in range(S)]
        zv = z.rearrange("h (p t) j -> t p h j", t=T)
        nc.scalar.dma_start(out=sv[:], in_=w_v_scale.rearrange("(p t) o -> p (t o)", t=T))
        nc.scalar.dma_start(out=gain[:], in_=ln_g.rearrange("(p t) -> p t", t=T))
        nc.scalar.dma_start(out=cst[0:4, :], in_=c)
        nc.scalar.dma_start(out=tv[:], in_=t.rearrange("s (p t) -> p s t", t=T))
        for k in range(2):
            nc.sync.dma_start(out=x[0][:, 2 * k : 2 * k + 2, :], in_=mv_[0][:, 2 * k : 2 * k + 2, :])
        nc.sync.dma_start(out=zt[0][:], in_=zv[0])
        nc.sync.dma_start(out=wv_bytes[:], in_=w_v_bytes.rearrange("(p t) n -> p t n", t=T))
        nc.sync.dma_start(out=x[1][:], in_=mv_[1])
        nc.sync.dma_start(out=wg_raw[:], in_=w_g.rearrange("(p t) n -> p t n", t=T))
        nc.sync.dma_start(out=zt[1][:], in_=zv[1])
        nc.sync.dma_start(out=zt[2][:], in_=zv[2])
        nc.sync.dma_start(out=zt[3][:], in_=zv[3])

        warm = sb([P, 1], F32, "warm")
        nc.vector.memset(warm[:], 0.0)
        nc.scalar.activation(out=warm[:], in_=warm[:], func=ACT.Exp)
        ident = sb([P, P], F32, "ident")
        make_identity(nc, ident[:])
        mhalf = sb([P, T], F32, "mhalf")
        nc.gpsimd.memset(mhalf[:], -0.5)
        csp = sb([P, D], BF16, "csp")
        nc.gpsimd.tensor_scalar(out=csp[:].rearrange("p (u q e) -> p u q e", u=2, e=2), in0=cst[:].rearrange("p (q u e) -> p u q e", u=2, e=2), scalar1=1.0, scalar2=1.0, op0=ALU.mult, op1=ALU.mult)
        sel = sb([P, 8], BF16, "sel")
        nc.vector.tensor_copy(out=sel[:], in_=ident[:, 0:8])
        th = sb([P, S, T], F32, "th")
        cb = [ps_c.tile([P, 2, R], BF16, name="cb%d" % k) for k in range(2)]

        def weave(*lanes):
            lanes = [list(l) for l in lanes]
            while any(lanes):
                for l in lanes:
                    if l:
                        l[0]()
                        l.remove(l[0])

        def run(*lanes):
            for l in lanes:
                for step in l:
                    step()

        def spread(h):
            nc.tensor.matmul(cb[h // 2][:, h % 2, :], lhsT=sel[:, h : h + 1].to_broadcast([P, P]), rhs=csp[:], start=True, stop=True)

        def quantize(codes, scales, src):
            nc.vector.quantize_mx(out=codes.bitcast(FP8X4), scales=scales, in_=src)

        st = [sb([P, T, 6], F32, "st%d" % s) for s in range(S)]
        mv = [sb([P, T, 2], F32, "mv%d" % s) for s in range(S)]
        ve = [sb([P, T], F32, "ve%d" % s) for s in range(S)]
        nmean = [sb([P, T], F32, "nmean%d" % s) for s in range(S)]
        rstd = [sb([P, T], F32, "rstd%d" % s) for s in range(S)]
        xn = [sb([P, T, D], F32, "xn%d" % s) for s in range(S)]
        mg = [sb([P, T * P * T], BF16, "mg%d" % s) for s in range(S)]
        mq = [sb([P, R], U32, "mq%d" % s) for s in range(S)]
        ms = [sb([P, R], U8, "ms%d" % s) for s in range(S)]

        def ln_stats(s):
            def bn(k):
                return lambda: nc.vector.bn_stats(out=st[s][:, k, :], in_=x[s][:, k, :])

            def agg(k):
                return lambda: nc.vector.bn_aggr(out=mv[s][:, k, :], in_=st[s][:, k, :])

            return [bn(k) for k in range(T)] + [agg(k) for k in range(T)]

        junk = sb([P, 2, D], BF16, "junk")
        tot = sb([P, 2], F32, "tot")
        ssq = sb([P, 2], F32, "ssq")

        def sum_s(k):
            nc.scalar.activation(out=junk[:, k - 2, :], in_=x[0][:, k, :], func=ACT.Copy, scale=1.0, accum_out=tot[:, k - 2 : k - 1])

        def mean_s():
            nc.gpsimd.tensor_scalar(out=nmean[0][:, 2:4], in0=tot[:], scalar1=-1.0 / D, scalar2=1.0, op0=ALU.mult, op1=ALU.mult)

        def square_s(k):
            nc.scalar.activation(out=junk[:, k - 2, :], in_=x[0][:, k, :], func=ACT.Square, scale=1.0, bias=nmean[0][:, k : k + 1], accum_out=ssq[:, k - 2 : k - 1])

        def ln_scales0():
            nc.gpsimd.tensor_scalar(out=nmean[0][:, 0:2], in0=mv[0][:, 0:2, 0], scalar1=-1.0, scalar2=1.0, op0=ALU.mult, op1=ALU.mult)
            nc.gpsimd.tensor_scalar(out=ve[0][:, 0:2], in0=mv[0][:, 0:2, 1], scalar1=1.0, scalar2=EPS, op0=ALU.mult, op1=ALU.add)
            nc.gpsimd.tensor_scalar(out=ve[0][:, 2:4], in0=ssq[:], scalar1=1.0 / D, scalar2=EPS, op0=ALU.mult, op1=ALU.add)
            nc.gpsimd.tensor_tensor(out=rstd[0][:], in0=ve[0][:], in1=mhalf[:], op=ALU.pow)

        def ln_scales(s):
            nc.gpsimd.tensor_scalar(out=ve[s][:], in0=mv[s][:, :, 1], scalar1=1.0, scalar2=EPS, op0=ALU.mult, op1=ALU.add)
            nc.gpsimd.tensor_tensor(out=rstd[s][:], in0=ve[s][:], in1=mhalf[:], op=ALU.pow)
            nc.gpsimd.tensor_scalar(out=nmean[s][:], in0=mv[s][:, :, 0], scalar1=-1.0, scalar2=1.0, op0=ALU.mult, op1=ALU.mult)

        nmr = [sb([P, T], F32, "nmr%d" % s) for s in range(S)]

        def ln_bias(s):
            nc.gpsimd.tensor_tensor(out=nmr[s][:], in0=nmean[s][:], in1=rstd[s][:], op=ALU.mult)

        def ln_norm(s, k):
            nc.scalar.activation(out=xn[s][:, k, :].rearrange("p (t q) -> p t q", t=T), in_=x[s][:, k, :].rearrange("p (q t) -> p t q", t=T),
                                 func=ACT.Identity, scale=rstd[s][:, k : k + 1], bias=nmr[s][:, k : k + 1])

        banks = {}

        def ln_turn(s, k):
            bank = ps_t.tile([P, T, P], F32, name="tr")
            for j in range(T):
                nc.tensor.transpose(bank[:, j, :], xn[s][:, k, j * P : (j + 1) * P], ident[:])
            banks[(s, k)] = bank

        def ln_gain(s, k):
            nc.vector.tensor_tensor(out=mg[s][:, k * 512 : (k + 1) * 512].rearrange("p (r t) -> p r t", t=T), in0=banks[(s, k)][:].rearrange("p t r -> p r t"),
                                    in1=gain[:].unsqueeze(1).to_broadcast([P, P, T]), op=ALU.mult)

        def ln_quant(s):
            quantize(mq[s][:], ms[s][:], mg[s][:])

        def turn(src, dst, b):
            words = src[:].bitcast(F32)
            bank = ps_t.tile([P, 2, 2, P], F32, name="tr")
            for i in range(2):
                for u in range(2):
                    w0 = 256 * (2 * b + i)
                    nc.tensor.transpose(bank[:, i, u, :], words[:, w0 + P * u : w0 + P * (u + 1)], ident[:])
            dv = dst[:, b * 1024 : (b + 1) * 1024].bitcast(F32).rearrange("p (i r u) -> p i r u", i=2, u=2)
            nc.scalar.copy(out=dv, in_=bank[:].rearrange("p i u r -> p i r u"))

        wv_w = sb([P, T, D], BF16, "wv_w")
        wv_g = sb([P, D * T], BF16, "wv_g")
        wv_q = sb([P, D], U32, "wv_q")
        wv_s = sb([P, D], U8, "wv_s")
        wg_g = sb([P, D * T], BF16, "wg_g")
        wg_q = sb([P, D], U32, "wg_q")
        wg_s = sb([P, D], U8, "wg_s")

        def inter_g(dst, src, k):
            nc.gpsimd.tensor_scalar(out=dst[:, k * 512 : (k + 1) * 512].rearrange("p (n t) -> p n t", t=T), in0=src[:, :, k * P : (k + 1) * P].rearrange("p t n -> p n t"),
                                    scalar1=1.0, scalar2=1.0, op0=ALU.mult, op1=ALU.mult)

        def inter_s(dst, src, k):
            nc.scalar.copy(out=dst[:, k * 512 : (k + 1) * 512].rearrange("p (n t) -> p n t", t=T), in_=src[:, :, k * P : (k + 1) * P].rearrange("p t n -> p n t"))

        def inter_v(dst, src, k):
            nc.vector.tensor_copy(out=dst[:, k * 512 : (k + 1) * 512].rearrange("p (n t) -> p n t", t=T), in_=src[:, :, k * P : (k + 1) * P].rearrange("p t n -> p n t"))

        def widen(k):
            nc.scalar.activation(out=wv_w[:, k, :], in_=wv_bytes[:, k, :].bitcast(FP8), func=ACT.Copy, scale=sv[:, k : k + 1])

        vg = [sb([P, D * T], BF16, "vg%d" % s) for s in range(S)]
        vq = [sb([P, D], U32, "vq%d" % s) for s in range(S)]
        vs = [sb([P, D], U8, "vs%d" % s) for s in range(S)]
        gt = [sb([P, T, D], F32, "gt%d" % s) for s in range(S)]

        def project(dst, s, k, wq, ws):
            cols = slice(k * P, (k + 1) * P)
            nc.tensor.matmul_mx(out=dst, lhsT=mq[s][:, cols].bitcast(FP8X4), lhsT_scale=ms[s][:, cols],
                                rhs=wq[:].bitcast(FP8X4), rhs_scale=ws[:], start=True, stop=True)

        vb = [sb([P, T, D], BF16, "vb%d" % s) for s in range(S)]

        def values(s, k):
            acc = ps_m.tile([P, D], F32, name="mm")
            project(acc[:], s, k, wv_q, wv_s)
            nc.scalar.activation(out=vb[s][:, k, :], in_=acc[:], func=ACT.Copy, scale=th[:, s, k : k + 1])

        def gate(s, k):
            acc = ps_m.tile([P, D], F32, name="mm")
            project(acc[:], s, k, wg_q, wg_s)
            nc.scalar.activation(out=gt[s][:, k, :], in_=acc[:], func=ACT.Tanh, scale=0.5)

        nm = [sb([P, H], F32, "nm%d" % i) for i in range(T)]
        sums = [sb([P, H], F32, "sums%d" % i) for i in range(T)]
        rs = [sb([P, H], F32, "rs%d" % i) for i in range(T)]
        ez = [sb([P, H, R], F32, "ez%d" % i) for i in range(T)]
        ab = [sb([P, H * R], BF16, "ab%d" % i) for i in range(T)]
        ag = [sb([P, H * P * T], BF16, "ag%d" % i) for i in range(T)]
        aq = [sb([P, H * P], U32, "aq%d" % i) for i in range(T)]
        asc = [sb([P, H * P], U8, "as%d" % i) for i in range(T)]
        osb = [[sb([P, D], F32, "o%d_%d" % (i, s)) for s in range(S)] for i in range(T)]

        zneg = sb([P, H, R], BF16, "zneg")

        def row_max(i):
            return [lambda h=h: nc.vector.tensor_scalar(out=zneg[:, h, :], in0=zt[i][:, h, :], scalar1=-1.0, scalar2=None, op0=ALU.mult, op1=ALU.min, accum_out=nm[i][:, h : h + 1]) for h in range(H)]

        def exps(i, h):
            nc.scalar.activation(out=ez[i][:, h, :].rearrange("p (u q e) -> p u q e", u=2, e=2), in_=zt[i][:, h, :].rearrange("p (q u e) -> p u q e", u=2, e=2), func=ACT.Exp, bias=nm[i][:, h : h + 1], scale=1.0, accum_out=sums[i][:, h : h + 1])

        def recip(i):
            nc.vector.reciprocal(out=rs[i][:], in_=sums[i][:])

        def weights(i, h):
            nc.vector.scalar_tensor_tensor(out=ab[i][:, h * R : (h + 1) * R], in0=ez[i][:, h, :], scalar=rs[i][:, h : h + 1], in1=cb[h // 2][:, h % 2, :], op0=ALU.mult, op1=ALU.mult)

        def a_quant(i):
            quantize(aq[i][:], asc[i][:], ag[i][:])

        def average(i, s):
            acc = ps_m.tile([P, D], F32, name="mm")
            for h in range(H):
                cols = slice(h * P, (h + 1) * P)
                nc.tensor.matmul_mx(out=acc[:, cols], lhsT=aq[i][:, cols].bitcast(FP8X4), lhsT_scale=asc[i][:, cols],
                                    rhs=vq[s][:, cols].bitcast(FP8X4), rhs_scale=vs[s][:, cols], start=True, stop=True)
            nc.vector.scalar_tensor_tensor(out=osb[i][s][:], in0=gt[s][:, i, :], scalar=1.0, in1=acc[:], op0=ALU.add, op1=ALU.mult)
            nc.sync.dma_start(out=out[s].rearrange("(p t) f -> p t f", t=T)[:, i, :], in_=osb[i][s][:])

        def halve_t():
            nc.vector.tensor_scalar(out=th[:], in0=tv[:], scalar1=0.5, scalar2=None, op0=ALU.mult)

        ctx.enter_context(tc.manual_schedule())
        run(ln_stats(0)[0:2] + ln_stats(0)[4:6])
        sum_s(2); sum_s(3); mean_s()
        spread(0); spread(1); spread(2); spread(3)
        run(row_max(0))
        run(ln_stats(1))
        square_s(2); square_s(3)
        exps(0, 0); exps(0, 1)
        run(row_max(1))
        exps(0, 2); exps(0, 3)
        ln_scales0(); ln_bias(0)
        ln_norm(0, 2); ln_norm(0, 3)
        recip(0)
        halve_t()
        widen(2); widen(3)
        ln_scales(1); ln_bias(1)
        ln_norm(0, 0); ln_norm(0, 1)
        ln_norm(1, 0); ln_norm(1, 1)
        widen(0); widen(1)
        ln_turn(0, 2); ln_gain(0, 2)
        ln_turn(0, 3); ln_gain(0, 3)
        ln_norm(1, 2); ln_norm(1, 3)
        weights(0, 0); weights(0, 1)
        ln_turn(0, 0); ln_gain(0, 0)
        ln_turn(0, 1); ln_gain(0, 1)
        exps(1, 2); exps(1, 3)
        exps(1, 0); exps(1, 1)
        run(row_max(2))
        ln_turn(1, 1); ln_gain(1, 1)
        weights(0, 2); weights(0, 3)
        ln_turn(1, 3); ln_gain(1, 3)
        ln_turn(1, 0); ln_gain(1, 0)
        ln_turn(1, 2); ln_gain(1, 2)
        inter_g(wg_g, wg_raw, 0); inter_g(wg_g, wg_raw, 1); inter_g(wg_g, wg_raw, 2); inter_g(wg_g, wg_raw, 3)
        ln_quant(0)
        inter_g(wv_g, wv_w, 0); inter_g(wv_g, wv_w, 1); inter_g(wv_g, wv_w, 2); inter_g(wv_g, wv_w, 3)
        exps(2, 2); exps(2, 3)
        quantize(wv_q[:], wv_s[:], wv_g[:])
        turn(ab[0], ag[0], 0)
        exps(2, 0); exps(2, 1)
        values(0, 3)
        turn(ab[0], ag[0], 1)
        ln_quant(1)
        values(0, 1)
        run(row_max(3))
        values(0, 2)
        recip(1)
        recip(2)
        weights(1, 0); weights(1, 1)
        values(0, 0)
        a_quant(0)
        exps(3, 0); exps(3, 1)
        quantize(wg_q[:], wg_s[:], wg_g[:])
        weights(1, 2); weights(1, 3)
        exps(3, 2); exps(3, 3)
        inter_g(vg[0], vb[0], 0); inter_g(vg[0], vb[0], 1); inter_g(vg[0], vb[0], 2); inter_g(vg[0], vb[0], 3)
        weights(2, 2); weights(2, 3)
        recip(3)
        values(1, 1)
        turn(ab[1], ag[1], 0)
        values(1, 3)
        weights(2, 0); weights(2, 1)
        turn(ab[1], ag[1], 1)
        values(1, 0)
        values(1, 2)
        inter_g(vg[1], vb[1], 0); inter_g(vg[1], vb[1], 1); inter_g(vg[1], vb[1], 2); inter_g(vg[1], vb[1], 3)
        gate(0, 1)
        quantize(vq[0][:], vs[0][:], vg[0][:])
        a_quant(1)
        turn(ab[2], ag[2], 0)
        gate(0, 0)
        turn(ab[2], ag[2], 1)
        gate(1, 2)
        weights(3, 0); weights(3, 1)
        weights(3, 2); weights(3, 3)
        average(1, 0)
        gate(0, 2)
        turn(ab[3], ag[3], 0)
        average(0, 0)
        a_quant(2)
        quantize(vq[1][:], vs[1][:], vg[1][:])
        turn(ab[3], ag[3], 1)
        gate(1, 0)
        gate(1, 3)
        gate(0, 3)
        a_quant(3)
        average(2, 0)
        average(2, 1)
        average(3, 1)
        average(0, 1)
        gate(1, 1)
        average(3, 0)
        average(1, 1)
